import numpy as np
import ml_dtypes


def mxq(x, axis, fmt="e4m3"):
    dtype, down = {"e4m3": (ml_dtypes.float8_e4m3fn, 7), "e5m2": (ml_dtypes.float8_e5m2, 14)}[fmt]
    v = np.moveaxis(np.asarray(x, np.float32).astype(ml_dtypes.bfloat16).astype(np.float64), axis, -1)
    blocks = v.reshape(v.shape[:-1] + (-1, 32))
    amax = np.abs(blocks).max(-1, keepdims=True)
    byte = np.maximum(np.where(amax > 0, np.frexp(amax)[1] - 1 + 127, 0) - down, 1)
    scale = np.exp2(byte - 127.0)
    codes = (blocks / scale).astype(np.float32).astype(dtype).astype(np.float64)
    return np.moveaxis((codes * scale).reshape(v.shape), -1, axis)


WIDE = False


def mx_kscale(k):
    if not WIDE:
        return np.ones(k)
    levels = np.array([10, -10, 5, -5, 0])
    if k % 512:
        return np.exp2(np.random.permutation(np.resize(levels, k // 32))).repeat(32)
    a = np.empty((k // 512, 16))
    for p in range(k // 512):
        a[p, :8] = np.random.permutation(np.resize(levels, 8))
        for g in range(8):
            far = levels[np.abs(levels - a[p, g]) >= 10]
            a[p, g + 8] = far[np.random.randint(len(far))]
    return np.exp2(a.ravel()).repeat(32)


def f64(x):
    return np.asarray(x).astype(np.float64)


def striped(idx):
    return np.tile(np.asarray(idx).reshape(-1, 16).T, (8, 1)).astype(np.uint16)


def unstriped(offs):
    return offs[:16].T.reshape(-1).astype(np.int64)


B, N, T, D, DV, NQ = 1, 512, 2048, 512, 512, 128


def setup_inputs():
    n = np.random.standard_normal
    idx = np.random.permutation(T)[:B * N]
    s = mx_kscale(D)[:, None]
    u = np.ones(T)
    u[idx] = mx_kscale(B * N)
    r = np.random.uniform(0.5, 2.0, T)
    k = n((D, T)) / s
    v = n((DV, T)) / (u * r)
    return {
        "qT": (n((B, D, NQ)) * s * (1.00 / np.sqrt(D))).astype(np.float32),
        "kT": k.astype(np.float32),
        "vT": v.astype(np.float32),
        "vs": np.tile(u * r, (128, 1)).astype(np.float32),
        "kb": np.tile(n(T), (128, 1)).astype(np.float32),
        "offs": striped(idx),
    }


def reference(qT, kT, vT, vs, kb, offs):
    idx = unstriped(offs)
    k = f64(kT)
    v = f64(vT)
    pick = lambda x: x[:, idx].reshape(x.shape[0], B, N).transpose(1, 0, 2)
    q = f64(qT)
    score = mxq(q, 1, "e4m3").transpose(0, 2, 1) @ mxq(pick(k), 1, "e4m3")
    score = score + pick(f64(kb))[:, :1, :]
    p = 1.0 / (1.0 + np.exp(-score))
    w = p * pick(f64(vs))[:, :1, :]
    y = mxq(w, 2, "e4m3") @ mxq(pick(v).transpose(0, 2, 1), 1, "e4m3")
    y = y / 16.0
    return y

@@ -1,0 +1,182 @@
+from contextlib import ExitStack
+
+import concourse.mybir as mybir
+from concourse.masks import make_identity
+
+NQ, D, T, N, DV = 128, 512, 2048, 512, 512
+P = 128
+PACK = 4
+LAST = P - 1
+E_BLOCKS = DV // P
+
+FLOPS = 2 * NQ * N * (D + DV)
+BYTES = 4 * (D * NQ + D * T + DV * T + 2 * T + NQ * DV) + 2 * P * (N // 16)
+
+F32 = mybir.dt.float32
+BF16 = mybir.dt.bfloat16
+U32 = mybir.dt.uint32
+U16 = mybir.dt.uint16
+U8 = mybir.dt.uint8
+FP8X4 = mybir.dt.float8_e4m3fn_x4
+ACT = mybir.ActivationFunctionType
+MULT = mybir.AluOpType.mult
+
+
+def tile_attend_sigmoid_topk_kernel(tc, qT, kT, vT, vs, kb, offs, out):
+    nc = tc.nc
+    with ExitStack() as ctx:
+        held = ctx.enter_context(tc.tile_pool(name="held", bufs=1))
+        psum2 = ctx.enter_context(tc.psum_pool(name="psum2", bufs=2))
+        psum1 = ctx.enter_context(tc.psum_pool(name="psum1", bufs=1))
+
+        offsets = held.tile([P, N // 16], U16, name="offsets")
+        nc.sync.dma_start(offsets[:], offs)
+
+        kb_win = held.tile([P, T], F32, name="kb_win")
+        vs_win = held.tile([P, T], F32, name="vs_win")
+        nc.gpsimd.memset(kb_win[0:LAST, :], 0.0)
+        nc.gpsimd.memset(vs_win[0:LAST, :], 0.0)
+        nc.sync.dma_start(kb_win[LAST:P, :], kb[LAST:P, :])
+        nc.sync.dma_start(vs_win[LAST:P, :], vs[LAST:P, :])
+
+        k_rows = kT.rearrange("(p j) n -> p j n", j=PACK)
+        k_win = []
+        for j in range(PACK):
+            win = held.tile([P, T], F32, name=f"k_win{j}")
+            nc.sync.dma_start(win[:], k_rows[:, j, :])
+            k_win.append(win)
+            if j == 1:
+                q_raw = held.tile([P, PACK, NQ], F32, name="q_raw")
+                nc.sync.dma_start(q_raw[:], qT[0].rearrange("(p j) q -> p j q", j=PACK))
+        v_win = []
+        for b in range(E_BLOCKS):
+            win = held.tile([P, T], F32, name=f"v_win{b}", tag=f"v_slot{b}", align_bytes=64)
+            nc.sync.dma_start(win[:], vT[b * P : (b + 1) * P, :])
+            v_win.append(win)
+
+        warm = held.tile([P, 1], F32, name="warm")
+        warm_out = held.tile([P, 1], F32, name="warm_out")
+        nc.vector.memset(warm[:], 0.0)
+        nc.scalar.activation(warm_out[:], warm[:], ACT.Sigmoid)
+        ident32 = held.tile([P, P], F32, name="ident32")
+        make_identity(nc, ident32[:])
+        ident16 = held.tile([P, P], BF16, name="ident16")
+        make_identity(nc, ident16[:])
+
+        k_grouped = held.tile([P, PACK, P, PACK], BF16, name="k_grouped", align_bytes=64)
+
+        def gather_key_plane(j):
+            nc.vector.tensor_copy(
+                k_grouped[:, :, :, j].rearrange("p t s -> p s t"),
+                k_win[j][:].indirect(offsets[:]),
+            )
+
+        def column(win, name):
+            g = held.tile([P, N], F32, name=name + "_g")
+            nc.vector.tensor_copy(g[:], win[:].indirect(offsets[:]))
+            turned = psum2.tile([P, PACK, P], F32, name="turned")
+            for t in range(PACK):
+                nc.tensor.transpose(turned[:, t, :], g[:, t::PACK], ident32[:])
+            col = held.tile([P, PACK], F32, name=name + "_col")
+            nc.scalar.copy(col[:], turned[:, :, LAST])
+            return col
+
+        gather_key_plane(0)
+        kb_col = column(kb_win, "kb")
+        gather_key_plane(1)
+        vs_col = column(vs_win, "vs")
+
+        q_grouped = held.tile([P, NQ, PACK], BF16, name="q_grouped", align_bytes=64)
+        nc.scalar.copy(q_grouped[:], q_raw[:].rearrange("p j q -> p q j"))
+        q_codes = held.tile([P, NQ], U32, name="q_codes", align_bytes=64)
+        q_scales = held.tile([P, NQ], U8, name="q_scales", align_bytes=64)
+        nc.vector.quantize_mx(
+            out=q_codes[:].bitcast(FP8X4), scales=q_scales[:], in_=q_grouped[:].rearrange("p q j -> p (q j)")
+        )
+
+        gather_key_plane(2)
+        gather_key_plane(3)
+        k_codes = held.tile([P, N], U32, name="k_codes", align_bytes=64)
+        k_scales = held.tile([P, N], U8, name="k_scales", align_bytes=64)
+        nc.vector.quantize_mx(
+            out=k_codes[:].bitcast(FP8X4),
+            scales=k_scales[:],
+            in_=k_grouped[:].rearrange("p t s j -> p (t s j)"),
+        )
+
+        scores = psum1.tile([P, PACK, NQ], F32, name="scores")
+        p_sig = held.tile([P, PACK, NQ], F32, name="p_sig")
+        for t in range(PACK):
+            cols = slice(t * P, (t + 1) * P)
+            nc.tensor.matmul_mx(
+                out=scores[:, t, :],
+                lhsT=k_codes[:, cols].bitcast(FP8X4),
+                lhsT_scale=k_scales[:, cols],
+                rhs=q_codes[:].bitcast(FP8X4),
+                rhs_scale=q_scales[:],
+                start=True,
+                stop=True,
+            )
+        for t in range(PACK):
+            nc.scalar.activation(p_sig[:, t, :], scores[:, t, :], ACT.Sigmoid, bias=kb_col[:, t : t + 1])
+
+        w_grouped = held.tile([P, NQ, PACK], BF16, name="w_grouped", align_bytes=64)
+        w_codes = held.tile([P, NQ], U32, name="w_codes", align_bytes=64)
+        w_scales = held.tile([P, NQ], U8, name="w_scales", align_bytes=64)
+
+        v_turned = []
+
+        def gather_values(b):
+            g = held.tile([P, PACK, P], BF16, name=f"v_gathered{b}", align_bytes=64)
+            nc.vector.tensor_copy(g[:].rearrange("p t s -> p s t"), v_win[b][:].indirect(offsets[:]))
+            turned = psum2.tile([P, PACK, P], BF16, name="v_turned")
+            for t in range(PACK):
+                nc.tensor.transpose(turned[:, t, :], g[:, t, :], ident16[:])
+            grouped = held.tile([P, P, PACK], BF16, name=f"v_grouped{b}", align_bytes=64)
+            for half in ([slice(0, P)] if b < E_BLOCKS - 1 else [slice(0, P // 2), slice(P // 2, P)]):
+                src = turned[:, :, half].rearrange("s t e -> s e t")
+                if half.start:
+                    nc.vector.tensor_copy(grouped[:, half, :], src)
+                else:
+                    nc.scalar.copy(grouped[:, half, :], src)
+            return grouped
+
+        def finish(b, grouped):
+            codes = held.tile([P, P], U32, name=f"v_codes{b}", tag=f"v_slot{b + 1}", align_bytes=64)
+            scales = held.tile([P, P], U8, name=f"v_scales{b}", align_bytes=64)
+            nc.vector.quantize_mx(
+                out=codes[:].bitcast(FP8X4), scales=scales[:], in_=grouped[:].rearrange("s e t -> s (e t)")
+            )
+            y = psum2.tile([NQ, P], F32, name="y")
+            nc.tensor.matmul_mx(
+                out=y[:],
+                lhsT=w_codes[:].bitcast(FP8X4),
+                lhsT_scale=w_scales[:],
+                rhs=codes[:].bitcast(FP8X4),
+                rhs_scale=scales[:],
+                start=True,
+                stop=True,
+            )
+            y_sb = held.tile([NQ, P], F32, name=f"y_sb{b}")
+            if b < 2:
+                nc.scalar.activation(y_sb[:], y[:], ACT.Copy, scale=1.0 / 16.0)
+            else:
+                nc.vector.tensor_scalar_mul(y_sb[:], y[:], 1.0 / 16.0)
+            nc.sync.dma_start(out[0][:, b * P : (b + 1) * P], y_sb[:])
+
+        g0 = gather_values(0)
+        nc.vector.tensor_tensor(
+            w_grouped[:],
+            p_sig[:].rearrange("s t q -> s q t"),
+            vs_col[:].unsqueeze(1).to_broadcast([P, NQ, PACK]),
+            MULT,
+        )
+        nc.vector.quantize_mx(
+            out=w_codes[:].bitcast(FP8X4), scales=w_scales[:], in_=w_grouped[:].rearrange("s q t -> s (q t)")
+        )
+        grouped = g0
+        for b in range(1, E_BLOCKS):
+            following = gather_values(b)
+            finish(b - 1, grouped)
+            grouped = following
+        finish(E_BLOCKS - 1, grouped)

@@ -30,14 +30,15 @@ def tile_attend_sigmoid_topk_kernel(tc, qT, kT, vT, vs, kb, offs, out):
         psum1 = ctx.enter_context(tc.psum_pool(name="psum1", bufs=1))
 
         offsets = held.tile([P, N // 16], U16, name="offsets")
-        nc.sync.dma_start(offsets[:], offs)
 
         kb_win = held.tile([P, T], F32, name="kb_win")
         vs_win = held.tile([P, T], F32, name="vs_win")
-        nc.gpsimd.memset(kb_win[0:LAST, :], 0.0)
-        nc.gpsimd.memset(vs_win[0:LAST, :], 0.0)
-        nc.sync.dma_start(kb_win[LAST:P, :], kb[LAST:P, :])
-        nc.sync.dma_start(vs_win[LAST:P, :], vs[LAST:P, :])
+        warm = held.tile([P, 1], F32, name="warm")
+        nc.vector.memset(warm[:], 0.0)
+        nc.vector.memset(kb_win[0:LAST, :], 0.0)
+        nc.vector.memset(vs_win[0:LAST, :], 0.0)
+        nc.scalar.dma_start(kb_win[LAST:P, :], kb[LAST:P, :])
+        nc.scalar.dma_start(vs_win[LAST:P, :], vs[LAST:P, :])
 
         k_rows = kT.rearrange("(p j) n -> p j n", j=PACK)
         k_win = []
@@ -45,7 +46,9 @@ def tile_attend_sigmoid_topk_kernel(tc, qT, kT, vT, vs, kb, offs, out):
             win = held.tile([P, T], F32, name=f"k_win{j}")
             nc.sync.dma_start(win[:], k_rows[:, j, :])
             k_win.append(win)
-            if j == 1:
+            if j == 0:
+                nc.sync.dma_start(offsets[:], offs)
+            if j == 2:
                 q_raw = held.tile([P, PACK, NQ], F32, name="q_raw")
                 nc.sync.dma_start(q_raw[:], qT[0].rearrange("(p j) q -> p j q", j=PACK))
         v_win = []
@@ -54,9 +57,7 @@ def tile_attend_sigmoid_topk_kernel(tc, qT, kT, vT, vs, kb, offs, out):
             nc.sync.dma_start(win[:], vT[b * P : (b + 1) * P, :])
             v_win.append(win)
 
-        warm = held.tile([P, 1], F32, name="warm")
         warm_out = held.tile([P, 1], F32, name="warm_out")
-        nc.vector.memset(warm[:], 0.0)
         nc.scalar.activation(warm_out[:], warm[:], ACT.Sigmoid)
         ident32 = held.tile([P, P], F32, name="ident32")
         make_identity(nc, ident32[:])

from contextlib import ExitStack

import concourse.mybir as mybir
from concourse.masks import make_identity

NQ, D, T, N, DV = 128, 512, 2048, 512, 512
P = 128
PACK = 4
LAST = P - 1
E_BLOCKS = DV // P

FLOPS = 2 * NQ * N * (D + DV)
BYTES = 4 * (D * NQ + D * T + DV * T + 2 * T + NQ * DV) + 2 * P * (N // 16)

F32 = mybir.dt.float32
BF16 = mybir.dt.bfloat16
U32 = mybir.dt.uint32
U16 = mybir.dt.uint16
U8 = mybir.dt.uint8
FP8X4 = mybir.dt.float8_e4m3fn_x4
ACT = mybir.ActivationFunctionType
MULT = mybir.AluOpType.mult


def tile_attend_sigmoid_topk_kernel(tc, qT, kT, vT, vs, kb, offs, out):
    nc = tc.nc
    with ExitStack() as ctx:
        held = ctx.enter_context(tc.tile_pool(name="held", bufs=1))
        psum2 = ctx.enter_context(tc.psum_pool(name="psum2", bufs=2))
        psum1 = ctx.enter_context(tc.psum_pool(name="psum1", bufs=1))

        offsets = held.tile([P, N // 16], U16, name="offsets")

        kb_win = held.tile([P, T], F32, name="kb_win")
        vs_win = held.tile([P, T], F32, name="vs_win")
        warm = held.tile([P, 1], F32, name="warm")
        nc.vector.memset(warm[:], 0.0)
        nc.vector.memset(kb_win[0:LAST, :], 0.0)
        nc.vector.memset(vs_win[0:LAST, :], 0.0)
        nc.scalar.dma_start(kb_win[LAST:P, :], kb[LAST:P, :])
        nc.scalar.dma_start(vs_win[LAST:P, :], vs[LAST:P, :])

        k_rows = kT.rearrange("(p j) n -> p j n", j=PACK)
        k_win = []
        for j in range(PACK):
            win = held.tile([P, T], F32, name=f"k_win{j}")
            nc.sync.dma_start(win[:], k_rows[:, j, :])
            k_win.append(win)
            if j == 0:
                nc.sync.dma_start(offsets[:], offs)
            if j == 2:
                q_raw = held.tile([P, PACK, NQ], F32, name="q_raw")
                nc.sync.dma_start(q_raw[:], qT[0].rearrange("(p j) q -> p j q", j=PACK))
        v_win = []
        for b in range(E_BLOCKS):
            win = held.tile([P, T], F32, name=f"v_win{b}", tag=f"v_slot{b}", align_bytes=64)
            nc.sync.dma_start(win[:], vT[b * P : (b + 1) * P, :])
            v_win.append(win)

        warm_out = held.tile([P, 1], F32, name="warm_out")
        nc.scalar.activation(warm_out[:], warm[:], ACT.Sigmoid)
        ident32 = held.tile([P, P], F32, name="ident32")
        make_identity(nc, ident32[:])
        ident16 = held.tile([P, P], BF16, name="ident16")
        make_identity(nc, ident16[:])

        k_grouped = held.tile([P, PACK, P, PACK], BF16, name="k_grouped", align_bytes=64)

        def gather_key_plane(j):
            nc.vector.tensor_copy(
                k_grouped[:, :, :, j].rearrange("p t s -> p s t"),
                k_win[j][:].indirect(offsets[:]),
            )

        def column(win, name):
            g = held.tile([P, N], F32, name=name + "_g")
            nc.vector.tensor_copy(g[:], win[:].indirect(offsets[:]))
            turned = psum2.tile([P, PACK, P], F32, name="turned")
            for t in range(PACK):
                nc.tensor.transpose(turned[:, t, :], g[:, t::PACK], ident32[:])
            col = held.tile([P, PACK], F32, name=name + "_col")
            nc.scalar.copy(col[:], turned[:, :, LAST])
            return col

        gather_key_plane(0)
        kb_col = column(kb_win, "kb")
        gather_key_plane(1)
        vs_col = column(vs_win, "vs")

        q_grouped = held.tile([P, NQ, PACK], BF16, name="q_grouped", align_bytes=64)
        nc.scalar.copy(q_grouped[:], q_raw[:].rearrange("p j q -> p q j"))
        q_codes = held.tile([P, NQ], U32, name="q_codes", align_bytes=64)
        q_scales = held.tile([P, NQ], U8, name="q_scales", align_bytes=64)
        nc.vector.quantize_mx(
            out=q_codes[:].bitcast(FP8X4), scales=q_scales[:], in_=q_grouped[:].rearrange("p q j -> p (q j)")
        )

        gather_key_plane(2)
        gather_key_plane(3)
        k_codes = held.tile([P, N], U32, name="k_codes", align_bytes=64)
        k_scales = held.tile([P, N], U8, name="k_scales", align_bytes=64)
        nc.vector.quantize_mx(
            out=k_codes[:].bitcast(FP8X4),
            scales=k_scales[:],
            in_=k_grouped[:].rearrange("p t s j -> p (t s j)"),
        )

        scores = psum1.tile([P, PACK, NQ], F32, name="scores")
        p_sig = held.tile([P, PACK, NQ], F32, name="p_sig")
        for t in range(PACK):
            cols = slice(t * P, (t + 1) * P)
            nc.tensor.matmul_mx(
                out=scores[:, t, :],
                lhsT=k_codes[:, cols].bitcast(FP8X4),
                lhsT_scale=k_scales[:, cols],
                rhs=q_codes[:].bitcast(FP8X4),
                rhs_scale=q_scales[:],
                start=True,
                stop=True,
            )
        for t in range(PACK):
            nc.scalar.activation(p_sig[:, t, :], scores[:, t, :], ACT.Sigmoid, bias=kb_col[:, t : t + 1])

        w_grouped = held.tile([P, NQ, PACK], BF16, name="w_grouped", align_bytes=64)
        w_codes = held.tile([P, NQ], U32, name="w_codes", align_bytes=64)
        w_scales = held.tile([P, NQ], U8, name="w_scales", align_bytes=64)

        v_turned = []

        def gather_values(b):
            g = held.tile([P, PACK, P], BF16, name=f"v_gathered{b}", align_bytes=64)
            nc.vector.tensor_copy(g[:].rearrange("p t s -> p s t"), v_win[b][:].indirect(offsets[:]))
            turned = psum2.tile([P, PACK, P], BF16, name="v_turned")
            for t in range(PACK):
                nc.tensor.transpose(turned[:, t, :], g[:, t, :], ident16[:])
            grouped = held.tile([P, P, PACK], BF16, name=f"v_grouped{b}", align_bytes=64)
            for half in ([slice(0, P)] if b < E_BLOCKS - 1 else [slice(0, P // 2), slice(P // 2, P)]):
                src = turned[:, :, half].rearrange("s t e -> s e t")
                if half.start:
                    nc.vector.tensor_copy(grouped[:, half, :], src)
                else:
                    nc.scalar.copy(grouped[:, half, :], src)
            return grouped

        def finish(b, grouped):
            codes = held.tile([P, P], U32, name=f"v_codes{b}", tag=f"v_slot{b + 1}", align_bytes=64)
            scales = held.tile([P, P], U8, name=f"v_scales{b}", align_bytes=64)
            nc.vector.quantize_mx(
                out=codes[:].bitcast(FP8X4), scales=scales[:], in_=grouped[:].rearrange("s e t -> s (e t)")
            )
            y = psum2.tile([NQ, P], F32, name="y")
            nc.tensor.matmul_mx(
                out=y[:],
                lhsT=w_codes[:].bitcast(FP8X4),
                lhsT_scale=w_scales[:],
                rhs=codes[:].bitcast(FP8X4),
                rhs_scale=scales[:],
                start=True,
                stop=True,
            )
            y_sb = held.tile([NQ, P], F32, name=f"y_sb{b}")
            if b < 2:
                nc.scalar.activation(y_sb[:], y[:], ACT.Copy, scale=1.0 / 16.0)
            else:
                nc.vector.tensor_scalar_mul(y_sb[:], y[:], 1.0 / 16.0)
            nc.sync.dma_start(out[0][:, b * P : (b + 1) * P], y_sb[:])

        g0 = gather_values(0)
        nc.vector.tensor_tensor(
            w_grouped[:],
            p_sig[:].rearrange("s t q -> s q t"),
            vs_col[:].unsqueeze(1).to_broadcast([P, NQ, PACK]),
            MULT,
        )
        nc.vector.quantize_mx(
            out=w_codes[:].bitcast(FP8X4), scales=w_scales[:], in_=w_grouped[:].rearrange("s q t -> s (q t)")
        )
        grouped = g0
        for b in range(1, E_BLOCKS):
            following = gather_values(b)
            finish(b - 1, grouped)
            grouped = following
        finish(E_BLOCKS - 1, grouped)
